import numpy as np
import ml_dtypes


def mxq(x, axis, fmt="e4m3"):
    dtype, down = {"e4m3": (ml_dtypes.float8_e4m3fn, 7), "e5m2": (ml_dtypes.float8_e5m2, 14)}[fmt]
    v = np.moveaxis(np.asarray(x, np.float32).astype(ml_dtypes.bfloat16).astype(np.float64), axis, -1)
    blocks = v.reshape(v.shape[:-1] + (-1, 32))
    amax = np.abs(blocks).max(-1, keepdims=True)
    byte = np.maximum(np.where(amax > 0, np.frexp(amax)[1] - 1 + 127, 0) - down, 1)
    scale = np.exp2(byte - 127.0)
    codes = (blocks / scale).astype(np.float32).astype(dtype).astype(np.float64)
    return np.moveaxis((codes * scale).reshape(v.shape), -1, axis)


WIDE = False


def mx_kscale(k):
    if not WIDE:
        return np.ones(k)
    levels = np.array([10, -10, 5, -5, 0])
    if k % 512:
        return np.exp2(np.random.permutation(np.resize(levels, k // 32))).repeat(32)
    a = np.empty((k // 512, 16))
    for p in range(k // 512):
        a[p, :8] = np.random.permutation(np.resize(levels, 8))
        for g in range(8):
            far = levels[np.abs(levels - a[p, g]) >= 10]
            a[p, g + 8] = far[np.random.randint(len(far))]
    return np.exp2(a.ravel()).repeat(32)


def f64(x):
    return np.asarray(x).astype(np.float64)


def striped8(idx):
    return np.asarray(idx).reshape(8, -1, 16).transpose(0, 2, 1).reshape(128, -1).astype(np.uint16)


def unstriped8(offs):
    return offs.reshape(8, 16, -1).transpose(0, 2, 1).reshape(8, -1).astype(np.int64)


def pick8(x, idx, run):
    r = np.arange(len(x))
    return x[r[:, None], idx[r % (8 * run) // run]]


E2M1 = np.array([0.0, 0.5, 1.0, 1.5, 2.0, 3.0, 4.0, 6.0, -0.0, -0.5, -1.0, -1.5, -2.0, -3.0, -4.0, -6.0])


def pack_weight(w, fmt):
    k, n = w.shape
    w = f64(np.asarray(w, np.float32).astype(ml_dtypes.bfloat16)).reshape(k // 32, 32, n)
    amax = np.abs(w).max(1)
    if fmt == "e4m3":
        byte = np.frexp(amax)[1] - 1 + 127 - 7
    else:
        mant, ex = np.frexp(amax / 6.0)
        byte = np.where(mant > 0.5, ex, ex - 1) + 127
    byte = np.clip(np.where(amax > 0, byte, 1), 1, 254)
    scaled = (w * np.exp2(127.0 - byte)[:, None, :]).reshape(k, n).astype(np.float32)
    by_word = np.ascontiguousarray(scaled.reshape(k // 512, 128, 4, n).transpose(0, 1, 3, 2))
    if fmt == "e4m3":
        words = by_word.astype(ml_dtypes.float8_e4m3fn).view(np.uint8)
    else:
        c = by_word.astype(ml_dtypes.float4_e2m1fn).view(np.uint8) & 0xF
        words = (c[..., 0::2] | (c[..., 1::2] << 4)).reshape(k // 512, 128, 2 * n)
    return np.ascontiguousarray(words), np.ascontiguousarray(byte.astype(np.uint8).reshape(k // 512, 16, n))


def unpack_weight(words, scales, fmt):
    g, _, n = scales.shape
    words = np.ascontiguousarray(words).reshape(g, 128, n, -1)
    if fmt == "e4m3":
        vals = words.view(ml_dtypes.float8_e4m3fn).astype(np.float64)
    else:
        nib = np.empty((g, 128, n, 4), np.uint8)
        nib[..., 0::2] = words & 0xF
        nib[..., 1::2] = words >> 4
        vals = E2M1[nib]
    vals = vals * np.repeat(np.exp2(scales.astype(np.float64) - 127.0), 8, axis=1)[..., None]
    return vals.transpose(0, 1, 3, 2).reshape(g * 512, n)


D, T, I, Q, E = 512, 1024, 512, 512, 256


def setup_inputs():
    n = np.random.standard_normal
    idx = np.stack([np.random.permutation(T)[:I] for _ in range(8)])
    idx2 = np.stack([np.random.permutation(T)[:I] for _ in range(8)])
    idx3 = np.stack([np.random.permutation(T)[:I] for _ in range(8)])
    idx4 = np.stack([np.random.permutation(T)[:I] for _ in range(8)])
    idx5 = np.stack([np.random.permutation(T)[:I] for _ in range(8)])
    idx6 = np.stack([np.random.permutation(T)[:I] for _ in range(8)])
    fd = mx_kscale(D)
    fq = mx_kscale(Q)
    keysp = pack_weight(n((D, T)) / fd[:, None], "e2m1")
    mixp = pack_weight(n((Q, E)) * 1.0 / np.sqrt(Q) / fq[:, None], "e4m3")
    return {
        "query": (n((D, Q)) * 1.0 / np.sqrt(D) * fd[:, None]).astype(np.float32),
        "keys_words": keysp[0],
        "keys_scales": keysp[1],
        "rowf": (np.random.uniform(0.5, 2.0, (Q, 1)) * fq[:, None]).astype(np.float32),
        "mix_words": mixp[0],
        "mix_scales": mixp[1],
        "offs": striped8(idx),
        "offs2": striped8(idx2),
        "offs3": striped8(idx3),
        "offs4": striped8(idx4),
        "offs5": striped8(idx5),
        "offs6": striped8(idx6),
    }


def reference(query, keys_words, keys_scales, rowf, mix_words, mix_scales, offs, offs2, offs3, offs4, offs5, offs6):
    idx = unstriped8(offs)
    idx2 = unstriped8(offs2)
    idx3 = unstriped8(offs3)
    idx4 = unstriped8(offs4)
    idx5 = unstriped8(offs5)
    idx6 = unstriped8(offs6)
    keysu = unpack_weight(keys_words, keys_scales, "e2m1")
    mixu = unpack_weight(mix_words, mix_scales, "e4m3")
    queryq = mxq(f64(query), 0, "e4m3")
    a = queryq.T @ keysu
    f1 = np.zeros((Q, T))
    f1[np.arange(Q)[:, None], idx3[np.arange(Q) % 512 // 64]] = pick8(a, idx, 64)
    f2 = np.zeros((Q, T))
    f2[np.arange(Q)[:, None], idx4[np.arange(Q) % 512 // 64]] = pick8(a, idx2, 64)
    r = np.maximum(f1, f2)
    cc = a + r
    g = pick8(cc, idx5, 64) - pick8(cc, idx6, 64)
    gw = g * f64(rowf)
    gwq = mxq(gw, 0, "e4m3")
    y = mixu.T @ gwq
    return y

@@ -1,0 +1,170 @@
+from contextlib import ExitStack
+
+import concourse.mybir as mybir
+
+D, T, I, Q, E = 512, 1024, 512, 512, 256
+FLOPS = 2 * D * Q * T + 2 * Q * E * I
+
+F32 = mybir.dt.float32
+BF16 = mybir.dt.bfloat16
+I32 = mybir.dt.int32
+U32 = mybir.dt.uint32
+U16 = mybir.dt.uint16
+U8 = mybir.dt.uint8
+FP8X4 = mybir.dt.float8_e4m3fn_x4
+FP4X4 = mybir.dt.float4_e2m1fn_x4
+ALU = mybir.AluOpType
+COPY = mybir.ActivationFunctionType.Copy
+
+P = 128
+PACK = 4
+BANK = 512
+HALF = I // 2
+LIST_HALF = HALF // 16
+
+
+def load_scale_rows(queue, plane, scales):
+    for quadrant in range(4):
+        queue.dma_start(
+            out=plane[32 * quadrant : 32 * quadrant + 4, :].bitcast(I32),
+            in_=scales[0, 4 * quadrant : 4 * quadrant + 4, :].bitcast(I32),
+        )
+
+
+def tile_attend_passedtwo_one_mixed_kernel(
+    tc, query, keys_words, keys_scales, rowf, mix_words, mix_scales, offs, offs2, offs3, offs4, offs5, offs6, out
+):
+    nc = tc.nc
+    last = PACK - 1
+    halves = [(slice(h * HALF, (h + 1) * HALF), slice(h * LIST_HALF, (h + 1) * LIST_HALF)) for h in range(2)]
+    with ExitStack() as ctx:
+        lists = ctx.enter_context(tc.tile_pool(name="lists", bufs=1))
+        keep = ctx.enter_context(tc.tile_pool(name="keep", bufs=1))
+        score_banks = ctx.enter_context(tc.psum_pool(name="score_banks", bufs=4))
+        out_banks = ctx.enter_context(tc.psum_pool(name="out_banks", bufs=1))
+
+        key_plane = keep.tile([P, T], U8, align_bytes=64)
+        mix_plane = keep.tile([P, E], U8, align_bytes=64)
+        nc.vector.memset(key_plane[:].bitcast(I32), 0)
+        nc.vector.memset(mix_plane[:].bitcast(I32), 0)
+
+        q_raw = keep.tile([P, PACK, Q], F32)
+        nc.sync.dma_start(out=q_raw[:], in_=query.rearrange("(p j) q -> p j q", j=PACK))
+        load_scale_rows(nc.scalar, key_plane, keys_scales)
+        key_words = keep.tile([P, 2 * T], U8, align_bytes=64)
+        nc.sync.dma_start(out=key_words[:].bitcast(I32), in_=keys_words[0].bitcast(I32))
+        idx = []
+        for n, source in enumerate((offs, offs2, offs3, offs4, offs5, offs6)):
+            idx.append(lists.tile([P, I // 16], U16, name="idx%d" % n))
+        for n in (0, 2, 1, 3, 4, 5):
+            nc.sync.dma_start(idx[n][:], (offs, offs2, offs3, offs4, offs5, offs6)[n])
+        take1, take2, put1, put2, take5, take6 = idx
+        factor = keep.tile([P, PACK], F32)
+        nc.sync.dma_start(out=factor[:], in_=rowf.rearrange("(p r) o -> p (r o)", r=PACK))
+        mix_codes = keep.tile([P, E], U32, align_bytes=64)
+        nc.sync.dma_start(out=mix_codes[:].bitcast(I32), in_=mix_words[0].rearrange("p n t -> p (n t)").bitcast(I32))
+        load_scale_rows(nc.sync, mix_plane, mix_scales)
+
+        f1 = [keep.tile([P, T], F32, name="f1_%d" % b) for b in range(2)]
+        f2 = [keep.tile([P, T], F32, name="f2_%d" % b) for b in range(2)]
+        for window in (f1[0], f2[0], f1[1], f2[1]):
+            nc.vector.memset(window[:], 0.0)
+
+        q_cols = q_raw[:].rearrange("p j (m r) -> p m j r", r=PACK)
+        q_first = keep.tile([P, P, PACK], BF16, align_bytes=64)
+        q_rest = keep.tile([P, last, P, PACK], BF16, align_bytes=64)
+        codes_first = keep.tile([P, P], U32, align_bytes=64)
+        plane_first = keep.tile([P, P], U8, align_bytes=64)
+        codes_rest = keep.tile([P, last * P], U32, align_bytes=64)
+        plane_rest = keep.tile([P, last * P], U8, align_bytes=64)
+        nc.vector.tensor_copy(out=q_first[:], in_=q_cols[:, :, :, 0])
+        nc.vector.quantize_mx(
+            out=codes_first[:].bitcast(FP8X4), scales=plane_first[:], in_=q_first[:].rearrange("p m j -> p (m j)")
+        )
+        nc.vector.tensor_copy(out=q_rest[:].rearrange("p r m j -> p m j r"), in_=q_cols[:, :, :, 1:PACK])
+        nc.vector.quantize_mx(
+            out=codes_rest[:].bitcast(FP8X4), scales=plane_rest[:], in_=q_rest[:].rearrange("p r m j -> p (r m j)")
+        )
+
+        a = [keep.tile([P, T], F32, name="a_%d" % r) for r in range(PACK)]
+        v1 = [keep.tile([P, I], F32, name="v1_%d" % r) for r in range(PACK)]
+        v2 = [keep.tile([P, I], F32, name="v2_%d" % r) for r in range(PACK)]
+        for r in range(PACK):
+            if r == 0:
+                codes, plane = codes_first[:], plane_first[:]
+            else:
+                codes, plane = codes_rest[:, (r - 1) * P : r * P], plane_rest[:, (r - 1) * P : r * P]
+            for b in range(T // BANK):
+                bank = score_banks.tile([P, BANK], F32, name="score")
+                nc.tensor.matmul_mx(
+                    out=bank[:],
+                    lhsT=codes.bitcast(FP8X4),
+                    lhsT_scale=plane,
+                    rhs=key_words[:, 2 * b * BANK : 2 * (b + 1) * BANK].bitcast(FP4X4),
+                    rhs_scale=key_plane[:, b * BANK : (b + 1) * BANK],
+                    start=True,
+                    stop=True,
+                )
+                nc.scalar.copy(out=a[r][:, b * BANK : (b + 1) * BANK], in_=bank[:])
+            if r == 0:
+                nc.vector.tensor_copy(v1[r][:, halves[0][0]], a[r][:].indirect(take1[:, halves[0][1]]))
+                nc.scalar.activation(v1[r][:, halves[1][0]], a[r][:].indirect(take1[:, halves[1][1]]), COPY)
+            else:
+                nc.scalar.activation(v1[r][:], a[r][:].indirect(take1[:]), COPY)
+            nc.scalar.activation(v2[r][:], a[r][:].indirect(take2[:]), COPY)
+
+        larger = [keep.tile([P, T], F32, name="larger_%d" % r) for r in range(PACK)]
+        cc = keep.tile([P, T], F32)
+        c5 = keep.tile([P, I], F32)
+        g = keep.tile([P, I], F32)
+        gw = keep.tile([P, I, PACK], BF16, align_bytes=64)
+        for r in range(PACK):
+            nc.vector.tensor_copy(f1[r % 2][:].indirect(put1[:]), v1[r][:])
+            nc.vector.tensor_copy(f2[r % 2][:].indirect(put2[:]), v2[r][:])
+            if r < last:
+                nc.vector.tensor_tensor(larger[r][:], f1[r % 2][:], f2[r % 2][:], ALU.max)
+                nc.gpsimd.tensor_tensor(cc[:], a[r][:], larger[r][:], ALU.add)
+                nc.scalar.activation(c5[:], cc[:].indirect(take5[:]), COPY)
+                nc.scalar.activation(g[:], cc[:].indirect(take6[:]), COPY)
+                nc.gpsimd.tensor_tensor(g[:], c5[:], g[:], ALU.subtract)
+                nc.scalar.activation(gw[:, :, r], g[:], COPY, scale=factor[:, r : r + 1])
+
+        cols = [slice(b * BANK, (b + 1) * BANK) for b in range(2)]
+        for c in cols:
+            nc.vector.tensor_tensor(larger[last][:, c], f1[last % 2][:, c], f2[last % 2][:, c], ALU.max)
+        for c in cols:
+            nc.vector.tensor_tensor(cc[:, c], a[last][:, c], larger[last][:, c], ALU.add)
+        for slots, entries in halves:
+            nc.vector.tensor_copy(c5[:, slots], cc[:].indirect(take5[:, entries]))
+            nc.scalar.activation(g[:, slots], cc[:].indirect(take6[:, entries]), COPY)
+        for slots, entries in halves:
+            nc.vector.tensor_tensor(g[:, slots], c5[:, slots], g[:, slots], ALU.subtract)
+        for slots, entries in halves:
+            nc.vector.tensor_scalar(gw[:, slots, last], g[:, slots], factor[:, last : last + 1], None, ALU.mult)
+        gw_codes = keep.tile([P, I], U32, align_bytes=64)
+        gw_plane = keep.tile([P, I], U8, align_bytes=64)
+        for slots, entries in halves:
+            nc.vector.quantize_mx(
+                out=gw_codes[:, slots].bitcast(FP8X4),
+                scales=gw_plane[:, slots],
+                in_=gw[:, slots, :].rearrange("p i r -> p (i r)"),
+            )
+        for h, (slots, entries) in enumerate(halves):
+            for block in range(E // P):
+                rows = slice(block * P, (block + 1) * P)
+                acc = out_banks.tile([P, HALF], F32, name="acc_%d_%d" % (h, block))
+                nc.tensor.matmul_mx(
+                    out=acc[:],
+                    lhsT=mix_codes[:, rows].bitcast(FP8X4),
+                    lhsT_scale=mix_plane[:, rows],
+                    rhs=gw_codes[:, slots].bitcast(FP8X4),
+                    rhs_scale=gw_plane[:, slots],
+                    start=True,
+                    stop=True,
+                )
+                result = keep.tile([P, HALF], F32, name="result_%d_%d" % (h, block))
+                if h == 1 and block == 1:
+                    nc.vector.tensor_copy(out=result[:], in_=acc[:])
+                else:
+                    nc.scalar.copy(out=result[:], in_=acc[:])
+                nc.sync.dma_start(out=out[rows, slots], in_=result[:])

@@ -15,6 +15,7 @@ FP8X4 = mybir.dt.float8_e4m3fn_x4
 FP4X4 = mybir.dt.float4_e2m1fn_x4
 ALU = mybir.AluOpType
 COPY = mybir.ActivationFunctionType.Copy
+RELU = mybir.ActivationFunctionType.Relu
 
 P = 128
 PACK = 4
@@ -48,8 +49,10 @@ def tile_attend_passedtwo_one_mixed_kernel(
         nc.vector.memset(key_plane[:].bitcast(I32), 0)
         nc.vector.memset(mix_plane[:].bitcast(I32), 0)
 
-        q_raw = keep.tile([P, PACK, Q], F32)
-        nc.sync.dma_start(out=q_raw[:], in_=query.rearrange("(p j) q -> p j q", j=PACK))
+        q_rows = query.rearrange("(p j) q -> p j q", j=PACK)
+        q_raw = [keep.tile([P, 2, Q], F32, name="q_raw_%d" % u) for u in range(2)]
+        for u in range(2):
+            nc.sync.dma_start(out=q_raw[u][:], in_=q_rows[:, 2 * u : 2 * u + 2, :])
         load_scale_rows(nc.scalar, key_plane, keys_scales)
         key_words = keep.tile([P, 2 * T], U8, align_bytes=64)
         nc.sync.dma_start(out=key_words[:].bitcast(I32), in_=keys_words[0].bitcast(I32))
@@ -67,21 +70,25 @@ def tile_attend_passedtwo_one_mixed_kernel(
 
         f1 = [keep.tile([P, T], F32, name="f1_%d" % b) for b in range(2)]
         f2 = [keep.tile([P, T], F32, name="f2_%d" % b) for b in range(2)]
-        for window in (f1[0], f2[0], f1[1], f2[1]):
+        for window in (f1[0], f2[0], f1[1]):
             nc.vector.memset(window[:], 0.0)
+        nc.gpsimd.memset(f2[1][:], 0.0)
 
-        q_cols = q_raw[:].rearrange("p j (m r) -> p m j r", r=PACK)
+        q_cols = [q_raw[u][:].rearrange("p j (m r) -> p m j r", r=PACK) for u in range(2)]
         q_first = keep.tile([P, P, PACK], BF16, align_bytes=64)
         q_rest = keep.tile([P, last, P, PACK], BF16, align_bytes=64)
         codes_first = keep.tile([P, P], U32, align_bytes=64)
         plane_first = keep.tile([P, P], U8, align_bytes=64)
         codes_rest = keep.tile([P, last * P], U32, align_bytes=64)
         plane_rest = keep.tile([P, last * P], U8, align_bytes=64)
-        nc.vector.tensor_copy(out=q_first[:], in_=q_cols[:, :, :, 0])
+        rest_view = q_rest[:].rearrange("p r m j -> p m j r")
+        nc.vector.tensor_copy(out=q_first[:, :, 0:2], in_=q_cols[0][:, :, :, 0])
+        nc.vector.tensor_copy(out=rest_view[:, :, 0:2, :], in_=q_cols[0][:, :, :, 1:PACK])
+        nc.vector.tensor_copy(out=q_first[:, :, 2:4], in_=q_cols[1][:, :, :, 0])
         nc.vector.quantize_mx(
             out=codes_first[:].bitcast(FP8X4), scales=plane_first[:], in_=q_first[:].rearrange("p m j -> p (m j)")
         )
-        nc.vector.tensor_copy(out=q_rest[:].rearrange("p r m j -> p m j r"), in_=q_cols[:, :, :, 1:PACK])
+        nc.vector.tensor_copy(out=rest_view[:, :, 2:4, :], in_=q_cols[1][:, :, :, 1:PACK])
         nc.vector.quantize_mx(
             out=codes_rest[:].bitcast(FP8X4), scales=plane_rest[:], in_=q_rest[:].rearrange("p r m j -> p (r m j)")
         )
@@ -89,23 +96,28 @@ def tile_attend_passedtwo_one_mixed_kernel(
         a = [keep.tile([P, T], F32, name="a_%d" % r) for r in range(PACK)]
         v1 = [keep.tile([P, I], F32, name="v1_%d" % r) for r in range(PACK)]
         v2 = [keep.tile([P, I], F32, name="v2_%d" % r) for r in range(PACK)]
-        for r in range(PACK):
+
+        def scores(r):
             if r == 0:
                 codes, plane = codes_first[:], plane_first[:]
+                pieces = [(0, 512, nc.scalar.copy), (512, 768, nc.vector.tensor_copy), (768, 1024, nc.scalar.copy)]
             else:
                 codes, plane = codes_rest[:, (r - 1) * P : r * P], plane_rest[:, (r - 1) * P : r * P]
-            for b in range(T // BANK):
-                bank = score_banks.tile([P, BANK], F32, name="score")
+                pieces = [(0, 512, nc.scalar.copy), (512, 1024, nc.scalar.copy)]
+            for lo, hi, empty in pieces:
+                bank = score_banks.tile([P, hi - lo], F32, name="score")
                 nc.tensor.matmul_mx(
                     out=bank[:],
                     lhsT=codes.bitcast(FP8X4),
                     lhsT_scale=plane,
-                    rhs=key_words[:, 2 * b * BANK : 2 * (b + 1) * BANK].bitcast(FP4X4),
-                    rhs_scale=key_plane[:, b * BANK : (b + 1) * BANK],
+                    rhs=key_words[:, 2 * lo : 2 * hi].bitcast(FP4X4),
+                    rhs_scale=key_plane[:, lo:hi],
                     start=True,
                     stop=True,
                 )
-                nc.scalar.copy(out=a[r][:, b * BANK : (b + 1) * BANK], in_=bank[:])
+                empty(out=a[r][:, lo:hi], in_=bank[:])
+
+        def pick(r):
             if r == 0:
                 nc.vector.tensor_copy(v1[r][:, halves[0][0]], a[r][:].indirect(take1[:, halves[0][1]]))
                 nc.scalar.activation(v1[r][:, halves[1][0]], a[r][:].indirect(take1[:, halves[1][1]]), COPY)
@@ -113,34 +125,90 @@ def tile_attend_passedtwo_one_mixed_kernel(
                 nc.scalar.activation(v1[r][:], a[r][:].indirect(take1[:]), COPY)
             nc.scalar.activation(v2[r][:], a[r][:].indirect(take2[:]), COPY)
 
-        larger = [keep.tile([P, T], F32, name="larger_%d" % r) for r in range(PACK)]
-        cc = keep.tile([P, T], F32)
-        c5 = keep.tile([P, I], F32)
-        g = keep.tile([P, I], F32)
-        gw = keep.tile([P, I, PACK], BF16, align_bytes=64)
-        for r in range(PACK):
-            nc.vector.tensor_copy(f1[r % 2][:].indirect(put1[:]), v1[r][:])
-            nc.vector.tensor_copy(f2[r % 2][:].indirect(put2[:]), v2[r][:])
-            if r < last:
-                nc.vector.tensor_tensor(larger[r][:], f1[r % 2][:], f2[r % 2][:], ALU.max)
-                nc.gpsimd.tensor_tensor(cc[:], a[r][:], larger[r][:], ALU.add)
-                nc.scalar.activation(c5[:], cc[:].indirect(take5[:]), COPY)
-                nc.scalar.activation(g[:], cc[:].indirect(take6[:]), COPY)
-                nc.gpsimd.tensor_tensor(g[:], c5[:], g[:], ALU.subtract)
-                nc.scalar.activation(gw[:, :, r], g[:], COPY, scale=factor[:, r : r + 1])
+        for r in range(last):
+            scores(r)
+            pick(r)
+        scores(last)
 
+        cc = [keep.tile([P, T], F32, name="cc_%d" % r) for r in range(last)]
+        partial = [keep.tile([P, T], F32, name="partial_%d" % r) for r in range(2)]
+        excess = [cc[2], cc[2]]
+        larger = [keep.tile([P, T], F32, name="larger_%d" % r) for r in range(2)]
+        c5s = [cc[1][:, 0:I]] + [keep.tile([P, I], F32, name="c5_%d" % r)[:] for r in range(1, PACK)]
+        c6s = [keep.tile([P, I], F32, name="c6_%d" % r) for r in range(last)]
+        gw = keep.tile([P, I, PACK], BF16, align_bytes=64)
+
+        def put_first(r):
+            nc.vector.tensor_copy(f1[r % 2][:].indirect(put1[:]), v1[r][:])
+
+        def put_second(r):
+            nc.vector.tensor_copy(f2[r % 2][:].indirect(put2[:]), v2[r][:])
+
+        def add_first(r):
+            nc.gpsimd.tensor_tensor(partial[r][:], a[r][:], f1[r % 2][:], ALU.add)
+
+        def difference(r):
+            nc.gpsimd.tensor_tensor(excess[r][:], f2[r % 2][:], f1[r % 2][:], ALU.subtract)
+
+        def clip(r):
+            nc.scalar.activation(excess[r][:], excess[r][:], RELU)
+
+        def add_excess(r):
+            nc.gpsimd.tensor_tensor(cc[r][:], partial[r][:], excess[r][:], ALU.add)
+
+        def look_up(r):
+            nc.scalar.activation(c5s[r], cc[r][:].indirect(take5[:]), COPY)
+            nc.scalar.activation(c6s[r][:], cc[r][:].indirect(take6[:]), COPY)
+
+        def subtract(r):
+            nc.gpsimd.tensor_tensor(c6s[r][:], c5s[r], c6s[r][:], ALU.subtract)
+
+        def weigh(r):
+            nc.scalar.activation(gw[:, :, r], c6s[r][:], COPY, scale=factor[:, r : r + 1])
+
+        put_first(0)
+        add_first(0)
+        put_second(0)
+        difference(0)
+        clip(0)
+        pick(last)
+        put_first(1)
+        add_first(1)
+        add_excess(0)
+        look_up(0)
+        put_second(1)
+        difference(1)
+        clip(1)
+        subtract(0)
+        weigh(0)
+        add_excess(1)
+        look_up(1)
+        put_first(2)
+        put_second(2)
+        nc.vector.tensor_tensor(larger[0][:], f1[0][:], f2[0][:], ALU.max)
+        nc.gpsimd.tensor_tensor(cc[2][:], a[2][:], larger[0][:], ALU.add)
+        look_up(2)
+        subtract(1)
+        weigh(1)
+        subtract(2)
+        weigh(2)
+        put_first(3)
+        put_second(3)
+
+        c5, c6 = c5s[last], c6s[2]
         cols = [slice(b * BANK, (b + 1) * BANK) for b in range(2)]
         for c in cols:
-            nc.vector.tensor_tensor(larger[last][:, c], f1[last % 2][:, c], f2[last % 2][:, c], ALU.max)
+            nc.vector.tensor_tensor(larger[1][:, c], f1[1][:, c], f2[1][:, c], ALU.max)
         for c in cols:
-            nc.vector.tensor_tensor(cc[:, c], a[last][:, c], larger[last][:, c], ALU.add)
+            nc.vector.tensor_tensor(cc[2][:, c], a[last][:, c], larger[1][:, c], ALU.add)
+        (slots_a, entries_a), (slots_b, entries_b) = halves
+        nc.scalar.activation(c6[:, slots_a], cc[2][:].indirect(take6[:, entries_a]), COPY)
+        nc.scalar.activation(c6[:, slots_b], cc[2][:].indirect(take6[:, entries_b]), COPY)
+        nc.vector.tensor_copy(c5[:, slots_b], cc[2][:].indirect(take5[:, entries_b]))
+        nc.vector.tensor_tensor(c5[:, slots_a], cc[2][:].indirect(take5[:, entries_a]), c6[:, slots_a], ALU.subtract)
+        nc.vector.tensor_tensor(c5[:, slots_b], c5[:, slots_b], c6[:, slots_b], ALU.subtract)
         for slots, entries in halves:
-            nc.vector.tensor_copy(c5[:, slots], cc[:].indirect(take5[:, entries]))
-            nc.scalar.activation(g[:, slots], cc[:].indirect(take6[:, entries]), COPY)
-        for slots, entries in halves:
-            nc.vector.tensor_tensor(g[:, slots], c5[:, slots], g[:, slots], ALU.subtract)
-        for slots, entries in halves:
-            nc.vector.tensor_scalar(gw[:, slots, last], g[:, slots], factor[:, last : last + 1], None, ALU.mult)
+            nc.vector.tensor_scalar(gw[:, slots, last], c5[:, slots], factor[:, last : last + 1], None, ALU.mult)
         gw_codes = keep.tile([P, I], U32, align_bytes=64)
         gw_plane = keep.tile([P, I], U8, align_bytes=64)
         for slots, entries in halves:
@@ -163,8 +231,9 @@ def tile_attend_passedtwo_one_mixed_kernel(
                     stop=True,
                 )
                 result = keep.tile([P, HALF], F32, name="result_%d_%d" % (h, block))
-                if h == 1 and block == 1:
+                if block == 1:
                     nc.vector.tensor_copy(out=result[:], in_=acc[:])
                 else:
                     nc.scalar.copy(out=result[:], in_=acc[:])
-                nc.sync.dma_start(out=out[rows, slots], in_=result[:])
+                queue = nc.scalar if (h, block) == (1, 0) else nc.sync
+                queue.dma_start(out=out[rows, slots], in_=result[:])

@@ -22,6 +22,7 @@ PACK = 4
 BANK = 512
 HALF = I // 2
 LIST_HALF = HALF // 16
+QUARTER = I // 4
 
 
 def load_scale_rows(queue, plane, scales):
@@ -93,11 +94,26 @@ def tile_attend_passedtwo_one_mixed_kernel(
             out=codes_rest[:].bitcast(FP8X4), scales=plane_rest[:], in_=q_rest[:].rearrange("p r m j -> p (r m j)")
         )
 
-        a = [keep.tile([P, T], F32, name="a_%d" % r) for r in range(PACK)]
-        v1 = [keep.tile([P, I], F32, name="v1_%d" % r) for r in range(PACK)]
-        v2 = [keep.tile([P, I], F32, name="v2_%d" % r) for r in range(PACK)]
+        place = (0, 2, 3, 1)
+        (slots_a, entries_a), (slots_b, entries_b) = halves
+        cols = [slice(b * BANK, (b + 1) * BANK) for b in range(2)]
+        a = [keep.tile([P, T], F32, name="a_%d" % s) for s in range(PACK)]
+        cc = [keep.tile([P, T], F32, name="cc_%d" % s) for s in range(last)]
+        partial = keep.tile([P, T], F32)
+        excess = cc[2]
+        larger = [keep.tile([P, T + QUARTER], F32, name="larger_0"), keep.tile([P, T], F32, name="larger_1")]
+        v1 = [keep.tile([P, I], F32, name="v1_%d" % s)[:] for s in range(last)]
+        v2 = [keep.tile([P, I], F32, name="v2_%d" % s)[:] for s in range(PACK)]
+        last_a = larger[0][:, T - QUARTER : T + QUARTER]
+        c5s = [cc[1][:, cols[0]]] + [keep.tile([P, I], F32, name="c5_%d" % s)[:] for s in range(1, PACK)]
+        c6s = [keep.tile([P, I], F32, name="c6_%d" % s)[:] for s in range(PACK)]
+        gs = [v2[last], c6s[1], c6s[2]]
+        last_b = c6s[0][:, slots_b]
+        first_gap = [v2[2], a[last][:, cols[1]]]
+        gw = keep.tile([P, I, PACK], BF16, align_bytes=64)
 
-        def scores(r):
+        def scores(s):
+            r = place[s]
             if r == 0:
                 codes, plane = codes_first[:], plane_first[:]
                 pieces = [(0, 512, nc.scalar.copy), (512, 768, nc.vector.tensor_copy), (768, 1024, nc.scalar.copy)]
@@ -115,100 +131,112 @@ def tile_attend_passedtwo_one_mixed_kernel(
                     start=True,
                     stop=True,
                 )
-                empty(out=a[r][:, lo:hi], in_=bank[:])
+                empty(out=a[s][:, lo:hi], in_=bank[:])
 
-        def pick(r):
-            if r == 0:
-                nc.vector.tensor_copy(v1[r][:, halves[0][0]], a[r][:].indirect(take1[:, halves[0][1]]))
-                nc.scalar.activation(v1[r][:, halves[1][0]], a[r][:].indirect(take1[:, halves[1][1]]), COPY)
+        def pick_first(s):
+            if s == 0:
+                nc.vector.tensor_copy(v1[s][:, slots_a], a[s][:].indirect(take1[:, entries_a]))
+                nc.scalar.activation(v1[s][:, slots_b], a[s][:].indirect(take1[:, entries_b]), COPY)
             else:
-                nc.scalar.activation(v1[r][:], a[r][:].indirect(take1[:]), COPY)
-            nc.scalar.activation(v2[r][:], a[r][:].indirect(take2[:]), COPY)
+                nc.scalar.activation(v1[s], a[s][:].indirect(take1[:]), COPY)
 
-        for r in range(last):
-            scores(r)
-            pick(r)
-        scores(last)
+        def pick_second(s):
+            nc.scalar.activation(v2[s], a[s][:].indirect(take2[:]), COPY)
 
-        cc = [keep.tile([P, T], F32, name="cc_%d" % r) for r in range(last)]
-        partial = [keep.tile([P, T], F32, name="partial_%d" % r) for r in range(2)]
-        excess = [cc[2], cc[2]]
-        larger = [keep.tile([P, T], F32, name="larger_%d" % r) for r in range(2)]
-        c5s = [cc[1][:, 0:I]] + [keep.tile([P, I], F32, name="c5_%d" % r)[:] for r in range(1, PACK)]
-        c6s = [keep.tile([P, I], F32, name="c6_%d" % r) for r in range(last)]
-        gw = keep.tile([P, I, PACK], BF16, align_bytes=64)
+        def put_first(s):
+            nc.vector.tensor_copy(f1[s % 2][:].indirect(put1[:]), v1[s])
 
-        def put_first(r):
-            nc.vector.tensor_copy(f1[r % 2][:].indirect(put1[:]), v1[r][:])
+        def put_second(s):
+            nc.vector.tensor_copy(f2[s % 2][:].indirect(put2[:]), v2[s])
 
-        def put_second(r):
-            nc.vector.tensor_copy(f2[r % 2][:].indirect(put2[:]), v2[r][:])
+        def add_first(s):
+            nc.gpsimd.tensor_tensor(partial[:], a[s][:], f1[s % 2][:], ALU.add)
 
-        def add_first(r):
-            nc.gpsimd.tensor_tensor(partial[r][:], a[r][:], f1[r % 2][:], ALU.add)
+        def difference(s, c, gap):
+            nc.gpsimd.tensor_tensor(gap, f2[s % 2][:, c], f1[s % 2][:, c], ALU.subtract)
 
-        def difference(r):
-            nc.gpsimd.tensor_tensor(excess[r][:], f2[r % 2][:], f1[r % 2][:], ALU.subtract)
+        def clip(c, gap):
+            nc.scalar.activation(excess[:, c], gap, RELU)
 
-        def clip(r):
-            nc.scalar.activation(excess[r][:], excess[r][:], RELU)
+        def add_excess(s, c):
+            nc.gpsimd.tensor_tensor(cc[s][:, c], partial[:, c], excess[:, c], ALU.add)
 
-        def add_excess(r):
-            nc.gpsimd.tensor_tensor(cc[r][:], partial[r][:], excess[r][:], ALU.add)
+        def look_up(s):
+            nc.scalar.activation(c5s[s], cc[s][:].indirect(take5[:]), COPY)
+            nc.scalar.activation(c6s[s], cc[s][:].indirect(take6[:]), COPY)
 
-        def look_up(r):
-            nc.scalar.activation(c5s[r], cc[r][:].indirect(take5[:]), COPY)
-            nc.scalar.activation(c6s[r][:], cc[r][:].indirect(take6[:]), COPY)
+        def subtract(s):
+            nc.gpsimd.tensor_tensor(gs[s], c5s[s], c6s[s], ALU.subtract)
 
-        def subtract(r):
-            nc.gpsimd.tensor_tensor(c6s[r][:], c5s[r], c6s[r][:], ALU.subtract)
+        def weigh(s, slots):
+            r = place[s]
+            nc.scalar.activation(gw[:, slots, r], gs[s][:, slots], COPY, scale=factor[:, r : r + 1])
 
-        def weigh(r):
-            nc.scalar.activation(gw[:, :, r], c6s[r][:], COPY, scale=factor[:, r : r + 1])
-
+        whole = slice(0, T)
+        every = slice(0, I)
+        for s in range(2):
+            scores(s)
+            pick_first(s)
+            pick_second(s)
+        scores(2)
+        pick_first(2)
         put_first(0)
         add_first(0)
         put_second(0)
-        difference(0)
-        clip(0)
-        pick(last)
+        for c, gap in zip(cols, first_gap):
+            difference(0, c, gap)
+        for c, gap in zip(cols, first_gap):
+            clip(c, gap)
+        for c in cols:
+            add_excess(0, c)
+        pick_second(2)
+        scores(last)
+        nc.scalar.activation(last_a, a[last][:].indirect(take1[:, entries_a]), COPY)
+        look_up(0)
         put_first(1)
         add_first(1)
-        add_excess(0)
-        look_up(0)
         put_second(1)
-        difference(1)
-        clip(1)
+        difference(1, whole, excess[:])
+        clip(whole, excess[:])
         subtract(0)
-        weigh(0)
-        add_excess(1)
+        weigh(0, every)
+        nc.scalar.activation(last_b, a[last][:].indirect(take1[:, entries_b]), COPY)
+        pick_second(last)
+        add_excess(1, whole)
         look_up(1)
         put_first(2)
         put_second(2)
-        nc.vector.tensor_tensor(larger[0][:], f1[0][:], f2[0][:], ALU.max)
-        nc.gpsimd.tensor_tensor(cc[2][:], a[2][:], larger[0][:], ALU.add)
-        look_up(2)
+        for lo in (0, QUARTER):
+            nc.vector.tensor_copy(f1[1][:].indirect(put1[:, lo // 16 : (lo + QUARTER) // 16]), last_a[:, lo : lo + QUARTER])
+        nc.vector.tensor_tensor(larger[0][:, whole], f1[0][:], f2[0][:], ALU.max)
+        nc.vector.tensor_copy(f1[1][:].indirect(put1[:, entries_b]), last_b)
+        nc.gpsimd.tensor_tensor(cc[2][:], a[2][:], larger[0][:, whole], ALU.add)
+        for slots, entries in halves:
+            nc.scalar.activation(c5s[2][:, slots], cc[2][:].indirect(take5[:, entries]), COPY)
+            nc.scalar.activation(c6s[2][:, slots], cc[2][:].indirect(take6[:, entries]), COPY)
         subtract(1)
-        weigh(1)
-        subtract(2)
-        weigh(2)
-        put_first(3)
+        nc.gpsimd.tensor_tensor(gs[2][:, slots_a], c5s[2][:, slots_a], c6s[2][:, slots_a], ALU.subtract)
+        weigh(1, every)
+        weigh(2, slots_a)
         put_second(3)
 
-        c5, c6 = c5s[last], c6s[2]
-        cols = [slice(b * BANK, (b + 1) * BANK) for b in range(2)]
+        c5 = c5s[last]
+        c6_a, c6_b = c6s[2][:, slots_a], c6s[last][:, slots_b]
         for c in cols:
             nc.vector.tensor_tensor(larger[1][:, c], f1[1][:, c], f2[1][:, c], ALU.max)
         for c in cols:
             nc.vector.tensor_tensor(cc[2][:, c], a[last][:, c], larger[1][:, c], ALU.add)
-        (slots_a, entries_a), (slots_b, entries_b) = halves
-        nc.scalar.activation(c6[:, slots_a], cc[2][:].indirect(take6[:, entries_a]), COPY)
-        nc.scalar.activation(c6[:, slots_b], cc[2][:].indirect(take6[:, entries_b]), COPY)
+        nc.scalar.activation(c6_a, cc[2][:].indirect(take6[:, entries_a]), COPY)
+        nc.scalar.activation(c6_b, cc[2][:].indirect(take6[:, entries_b]), COPY)
+        late_g = larger[1][:, T - HALF : T]
+        nc.gpsimd.tensor_tensor(late_g, c5s[2][:, slots_b], c6s[2][:, slots_b], ALU.subtract)
+        nc.scalar.activation(gw[:, slots_b, place[2]], late_g, COPY, scale=factor[:, place[2] : place[2] + 1])
         nc.vector.tensor_copy(c5[:, slots_b], cc[2][:].indirect(take5[:, entries_b]))
-        nc.vector.tensor_tensor(c5[:, slots_a], cc[2][:].indirect(take5[:, entries_a]), c6[:, slots_a], ALU.subtract)
-        nc.vector.tensor_tensor(c5[:, slots_b], c5[:, slots_b], c6[:, slots_b], ALU.subtract)
+        nc.vector.tensor_tensor(c5[:, slots_a], cc[2][:].indirect(take5[:, entries_a]), c6_a, ALU.subtract)
+        nc.vector.tensor_tensor(c5[:, slots_b], c5[:, slots_b], c6_b, ALU.subtract)
+        r = place[last]
         for slots, entries in halves:
-            nc.vector.tensor_scalar(gw[:, slots, last], c5[:, slots], factor[:, last : last + 1], None, ALU.mult)
+            nc.vector.tensor_scalar(gw[:, slots, r], c5[:, slots], factor[:, r : r + 1], None, ALU.mult)
         gw_codes = keep.tile([P, I], U32, align_bytes=64)
         gw_plane = keep.tile([P, I], U8, align_bytes=64)
         for slots, entries in halves:

@@ -89,7 +89,7 @@ def tile_attend_passedtwo_one_mixed_kernel(
         nc.vector.quantize_mx(
             out=codes_first[:].bitcast(FP8X4), scales=plane_first[:], in_=q_first[:].rearrange("p m j -> p (m j)")
         )
-        nc.vector.tensor_copy(out=rest_view[:, :, 2:4, :], in_=q_cols[1][:, :, :, 1:PACK])
+        nc.scalar.copy(out=rest_view[:, :, 2:4, :], in_=q_cols[1][:, :, :, 1:PACK])
         nc.vector.quantize_mx(
             out=codes_rest[:].bitcast(FP8X4), scales=plane_rest[:], in_=q_rest[:].rearrange("p r m j -> p (r m j)")
         )
@@ -116,7 +116,7 @@ def tile_attend_passedtwo_one_mixed_kernel(
             r = place[s]
             if r == 0:
                 codes, plane = codes_first[:], plane_first[:]
-                pieces = [(0, 512, nc.scalar.copy), (512, 768, nc.vector.tensor_copy), (768, 1024, nc.scalar.copy)]
+                pieces = [(0, 512, nc.scalar.copy), (512, 768, nc.vector.tensor_copy), (768, 896, nc.scalar.copy), (896, 1024, nc.vector.tensor_copy)]
             else:
                 codes, plane = codes_rest[:, (r - 1) * P : r * P], plane_rest[:, (r - 1) * P : r * P]
                 pieces = [(0, 512, nc.scalar.copy), (512, 1024, nc.scalar.copy)]

@@ -20,9 +20,12 @@ RELU = mybir.ActivationFunctionType.Relu
 P = 128
 PACK = 4
 BANK = 512
+STRIPE = 16
 HALF = I // 2
-LIST_HALF = HALF // 16
 QUARTER = I // 4
+PLACE = (0, 2, 3, 1)
+LAST = PACK - 1
+SCORE_BANKS = 4
 
 
 def load_scale_rows(queue, plane, scales):
@@ -33,36 +36,41 @@ def load_scale_rows(queue, plane, scales):
         )
 
 
+def entries_of(slots):
+    return slice(slots.start // STRIPE, slots.stop // STRIPE)
+
+
 def tile_attend_passedtwo_one_mixed_kernel(
     tc, query, keys_words, keys_scales, rowf, mix_words, mix_scales, offs, offs2, offs3, offs4, offs5, offs6, out
 ):
     nc = tc.nc
-    last = PACK - 1
-    halves = [(slice(h * HALF, (h + 1) * HALF), slice(h * LIST_HALF, (h + 1) * LIST_HALF)) for h in range(2)]
+    all_slots, slots_a, slots_b = slice(0, I), slice(0, HALF), slice(HALF, I)
+    all_tokens = slice(0, T)
+    token_halves = [slice(b * BANK, (b + 1) * BANK) for b in range(T // BANK)]
     with ExitStack() as ctx:
         lists = ctx.enter_context(tc.tile_pool(name="lists", bufs=1))
         keep = ctx.enter_context(tc.tile_pool(name="keep", bufs=1))
-        score_banks = ctx.enter_context(tc.psum_pool(name="score_banks", bufs=4))
+        score_banks = ctx.enter_context(tc.psum_pool(name="score_banks", bufs=SCORE_BANKS))
         out_banks = ctx.enter_context(tc.psum_pool(name="out_banks", bufs=1))
 
         key_plane = keep.tile([P, T], U8, align_bytes=64)
         mix_plane = keep.tile([P, E], U8, align_bytes=64)
-        nc.vector.memset(key_plane[:].bitcast(I32), 0)
-        nc.vector.memset(mix_plane[:].bitcast(I32), 0)
+        load_scale_rows(nc.scalar, key_plane, keys_scales)
 
         q_rows = query.rearrange("(p j) q -> p j q", j=PACK)
         q_raw = [keep.tile([P, 2, Q], F32, name="q_raw_%d" % u) for u in range(2)]
         for u in range(2):
             nc.sync.dma_start(out=q_raw[u][:], in_=q_rows[:, 2 * u : 2 * u + 2, :])
-        load_scale_rows(nc.scalar, key_plane, keys_scales)
-        key_words = keep.tile([P, 2 * T], U8, align_bytes=64)
-        nc.sync.dma_start(out=key_words[:].bitcast(I32), in_=keys_words[0].bitcast(I32))
-        idx = []
-        for n, source in enumerate((offs, offs2, offs3, offs4, offs5, offs6)):
-            idx.append(lists.tile([P, I // 16], U16, name="idx%d" % n))
-        for n in (0, 2, 1, 3, 4, 5):
-            nc.sync.dma_start(idx[n][:], (offs, offs2, offs3, offs4, offs5, offs6)[n])
-        take1, take2, put1, put2, take5, take6 = idx
+        key_words = [keep.tile([P, 2 * BANK], U8, align_bytes=64, name="key_words_%d" % b) for b in range(T // BANK)]
+        for b, words in enumerate(key_words):
+            nc.sync.dma_start(
+                out=words[:].bitcast(I32), in_=keys_words[0][:, 2 * b * BANK : 2 * (b + 1) * BANK].bitcast(I32)
+            )
+        take1, take2, put1, put2, take5, take6 = [
+            lists.tile([P, I // STRIPE], U16, name="list_%d" % n) for n in range(6)
+        ]
+        for held, source in ((take1, offs), (put1, offs3), (take2, offs2), (put2, offs4), (take5, offs5), (take6, offs6)):
+            nc.sync.dma_start(held[:], source)
         factor = keep.tile([P, PACK], F32)
         nc.sync.dma_start(out=factor[:], in_=rowf.rearrange("(p r) o -> p (r o)", r=PACK))
         mix_codes = keep.tile([P, E], U32, align_bytes=64)
@@ -77,11 +85,11 @@ def tile_attend_passedtwo_one_mixed_kernel(
 
         q_cols = [q_raw[u][:].rearrange("p j (m r) -> p m j r", r=PACK) for u in range(2)]
         q_first = keep.tile([P, P, PACK], BF16, align_bytes=64)
-        q_rest = keep.tile([P, last, P, PACK], BF16, align_bytes=64)
+        q_rest = keep.tile([P, LAST, P, PACK], BF16, align_bytes=64)
         codes_first = keep.tile([P, P], U32, align_bytes=64)
         plane_first = keep.tile([P, P], U8, align_bytes=64)
-        codes_rest = keep.tile([P, last * P], U32, align_bytes=64)
-        plane_rest = keep.tile([P, last * P], U8, align_bytes=64)
+        codes_rest = keep.tile([P, LAST * P], U32, align_bytes=64)
+        plane_rest = keep.tile([P, LAST * P], U8, align_bytes=64)
         rest_view = q_rest[:].rearrange("p r m j -> p m j r")
         nc.vector.tensor_copy(out=q_first[:, :, 0:2], in_=q_cols[0][:, :, :, 0])
         nc.vector.tensor_copy(out=rest_view[:, :, 0:2, :], in_=q_cols[0][:, :, :, 1:PACK])
@@ -94,174 +102,181 @@ def tile_attend_passedtwo_one_mixed_kernel(
             out=codes_rest[:].bitcast(FP8X4), scales=plane_rest[:], in_=q_rest[:].rearrange("p r m j -> p (r m j)")
         )
 
-        place = (0, 2, 3, 1)
-        (slots_a, entries_a), (slots_b, entries_b) = halves
-        cols = [slice(b * BANK, (b + 1) * BANK) for b in range(2)]
         a = [keep.tile([P, T], F32, name="a_%d" % s) for s in range(PACK)]
-        cc = [keep.tile([P, T], F32, name="cc_%d" % s) for s in range(last)]
+        cc_tiles = [keep.tile([P, T], F32, name="cc_%d" % s) for s in range(LAST)]
+        cc = cc_tiles + [cc_tiles[2]]
         partial = keep.tile([P, T], F32)
-        excess = cc[2]
-        larger = [keep.tile([P, T + QUARTER], F32, name="larger_0"), keep.tile([P, T], F32, name="larger_1")]
-        v1 = [keep.tile([P, I], F32, name="v1_%d" % s)[:] for s in range(last)]
-        v2 = [keep.tile([P, I], F32, name="v2_%d" % s)[:] for s in range(PACK)]
-        last_a = larger[0][:, T - QUARTER : T + QUARTER]
-        c5s = [cc[1][:, cols[0]]] + [keep.tile([P, I], F32, name="c5_%d" % s)[:] for s in range(1, PACK)]
-        c6s = [keep.tile([P, I], F32, name="c6_%d" % s)[:] for s in range(PACK)]
-        gs = [v2[last], c6s[1], c6s[2]]
-        last_b = c6s[0][:, slots_b]
-        first_gap = [v2[2], a[last][:, cols[1]]]
+        excess = cc_tiles[2]
+        larger = {2: keep.tile([P, T + QUARTER], F32, name="larger_2"), 3: keep.tile([P, T], F32, name="larger_3")}
+        picked1 = [keep.tile([P, I], F32, name="picked1_%d" % s)[:] for s in range(LAST)]
+        picked2 = [keep.tile([P, I], F32, name="picked2_%d" % s)[:] for s in range(PACK)]
+        last_picked1_a = larger[2][:, T - QUARTER : T + QUARTER]
+        c5 = [cc[1][:, all_slots]] + [keep.tile([P, I], F32, name="c5_%d" % s)[:] for s in range(1, PACK)]
+        c6 = [keep.tile([P, I], F32, name="c6_%d" % s)[:] for s in range(PACK)]
+        g = [picked2[LAST], c6[1], c6[2]]
+        last_picked1_b = c6[0][:, slots_b]
+        first_gap = [picked2[2], a[LAST][:, token_halves[1]]]
         gw = keep.tile([P, I, PACK], BF16, align_bytes=64)
 
         def scores(s):
-            r = place[s]
-            if r == 0:
+            r = PLACE[s]
+            if s == 0:
                 codes, plane = codes_first[:], plane_first[:]
-                pieces = [(0, 512, nc.scalar.copy), (512, 768, nc.vector.tensor_copy), (768, 896, nc.scalar.copy), (896, 1024, nc.vector.tensor_copy)]
+                pieces = [
+                    (0, 512, nc.scalar.copy),
+                    (512, 768, nc.vector.tensor_copy),
+                    (768, 896, nc.scalar.copy),
+                    (896, 1024, nc.vector.tensor_copy),
+                ]
             else:
                 codes, plane = codes_rest[:, (r - 1) * P : r * P], plane_rest[:, (r - 1) * P : r * P]
-                pieces = [(0, 512, nc.scalar.copy), (512, 1024, nc.scalar.copy)]
+                pieces = [(tokens.start, tokens.stop, nc.scalar.copy) for tokens in token_halves]
             for lo, hi, empty in pieces:
                 bank = score_banks.tile([P, hi - lo], F32, name="score")
                 nc.tensor.matmul_mx(
                     out=bank[:],
                     lhsT=codes.bitcast(FP8X4),
                     lhsT_scale=plane,
-                    rhs=key_words[:, 2 * lo : 2 * hi].bitcast(FP4X4),
+                    rhs=key_words[lo // BANK][:, 2 * (lo % BANK) : 2 * (lo % BANK + hi - lo)].bitcast(FP4X4),
                     rhs_scale=key_plane[:, lo:hi],
                     start=True,
                     stop=True,
                 )
                 empty(out=a[s][:, lo:hi], in_=bank[:])
 
-        def pick_first(s):
-            if s == 0:
-                nc.vector.tensor_copy(v1[s][:, slots_a], a[s][:].indirect(take1[:, entries_a]))
-                nc.scalar.activation(v1[s][:, slots_b], a[s][:].indirect(take1[:, entries_b]), COPY)
-            else:
-                nc.scalar.activation(v1[s], a[s][:].indirect(take1[:]), COPY)
+        def gather(dense, window, held, slots):
+            nc.scalar.activation(dense, window[:].indirect(held[:, entries_of(slots)]), COPY)
 
-        def pick_second(s):
-            nc.scalar.activation(v2[s], a[s][:].indirect(take2[:]), COPY)
+        def scatter(window, held, slots, dense):
+            nc.vector.tensor_copy(window[:].indirect(held[:, entries_of(slots)]), dense)
 
         def put_first(s):
-            nc.vector.tensor_copy(f1[s % 2][:].indirect(put1[:]), v1[s])
+            scatter(f1[s % 2], put1, all_slots, picked1[s])
 
         def put_second(s):
-            nc.vector.tensor_copy(f2[s % 2][:].indirect(put2[:]), v2[s])
+            scatter(f2[s % 2], put2, all_slots, picked2[s])
 
         def add_first(s):
             nc.gpsimd.tensor_tensor(partial[:], a[s][:], f1[s % 2][:], ALU.add)
 
-        def difference(s, c, gap):
-            nc.gpsimd.tensor_tensor(gap, f2[s % 2][:, c], f1[s % 2][:, c], ALU.subtract)
+        def difference(s, tokens, gap):
+            nc.gpsimd.tensor_tensor(gap, f2[s % 2][:, tokens], f1[s % 2][:, tokens], ALU.subtract)
 
-        def clip(c, gap):
-            nc.scalar.activation(excess[:, c], gap, RELU)
+        def clip(tokens, gap):
+            nc.scalar.activation(excess[:, tokens], gap, RELU)
 
-        def add_excess(s, c):
-            nc.gpsimd.tensor_tensor(cc[s][:, c], partial[:, c], excess[:, c], ALU.add)
+        def add_excess(s, tokens):
+            nc.gpsimd.tensor_tensor(cc[s][:, tokens], partial[:, tokens], excess[:, tokens], ALU.add)
 
-        def look_up(s):
-            nc.scalar.activation(c5s[s], cc[s][:].indirect(take5[:]), COPY)
-            nc.scalar.activation(c6s[s], cc[s][:].indirect(take6[:]), COPY)
+        def maximum(s, tokens):
+            nc.vector.tensor_tensor(larger[s][:, tokens], f1[s % 2][:, tokens], f2[s % 2][:, tokens], ALU.max)
 
-        def subtract(s):
-            nc.gpsimd.tensor_tensor(gs[s], c5s[s], c6s[s], ALU.subtract)
+        def look_up(s, slots):
+            gather(c5[s][:, slots], cc[s], take5, slots)
+            gather(c6[s][:, slots], cc[s], take6, slots)
 
-        def weigh(s, slots):
-            r = place[s]
-            nc.scalar.activation(gw[:, slots, r], gs[s][:, slots], COPY, scale=factor[:, r : r + 1])
+        def subtract(result, s, slots):
+            nc.gpsimd.tensor_tensor(result, c5[s][:, slots], c6[s][:, slots], ALU.subtract)
 
-        whole = slice(0, T)
-        every = slice(0, I)
-        for s in range(2):
-            scores(s)
-            pick_first(s)
-            pick_second(s)
+        def weigh(values, s, slots):
+            r = PLACE[s]
+            nc.scalar.activation(gw[:, slots, r], values, COPY, scale=factor[:, r : r + 1])
+
+        scores(0)
+        nc.vector.tensor_copy(picked1[0][:, slots_a], a[0][:].indirect(take1[:, entries_of(slots_a)]))
+        gather(picked1[0][:, slots_b], a[0], take1, slots_b)
+        gather(picked2[0], a[0], take2, all_slots)
+        scores(1)
+        gather(picked1[1], a[1], take1, all_slots)
+        gather(picked2[1], a[1], take2, all_slots)
         scores(2)
-        pick_first(2)
+        gather(picked1[2], a[2], take1, all_slots)
+
         put_first(0)
         add_first(0)
         put_second(0)
-        for c, gap in zip(cols, first_gap):
-            difference(0, c, gap)
-        for c, gap in zip(cols, first_gap):
-            clip(c, gap)
-        for c in cols:
-            add_excess(0, c)
-        pick_second(2)
-        scores(last)
-        nc.scalar.activation(last_a, a[last][:].indirect(take1[:, entries_a]), COPY)
-        look_up(0)
+        for tokens, gap in zip(token_halves, first_gap):
+            difference(0, tokens, gap)
+        for tokens, gap in zip(token_halves, first_gap):
+            clip(tokens, gap)
+        for tokens in token_halves:
+            add_excess(0, tokens)
+        gather(picked2[2], a[2], take2, all_slots)
+        scores(LAST)
+        gather(last_picked1_a, a[LAST], take1, slots_a)
+        look_up(0, all_slots)
+
         put_first(1)
         add_first(1)
         put_second(1)
-        difference(1, whole, excess[:])
-        clip(whole, excess[:])
-        subtract(0)
-        weigh(0, every)
-        nc.scalar.activation(last_b, a[last][:].indirect(take1[:, entries_b]), COPY)
-        pick_second(last)
-        add_excess(1, whole)
-        look_up(1)
+        difference(1, all_tokens, excess[:])
+        clip(all_tokens, excess[:])
+        subtract(g[0], 0, all_slots)
+        weigh(g[0], 0, all_slots)
+        gather(last_picked1_b, a[LAST], take1, slots_b)
+        gather(picked2[LAST], a[LAST], take2, all_slots)
+        add_excess(1, all_tokens)
+        look_up(1, all_slots)
+
         put_first(2)
         put_second(2)
         for lo in (0, QUARTER):
-            nc.vector.tensor_copy(f1[1][:].indirect(put1[:, lo // 16 : (lo + QUARTER) // 16]), last_a[:, lo : lo + QUARTER])
-        nc.vector.tensor_tensor(larger[0][:, whole], f1[0][:], f2[0][:], ALU.max)
-        nc.vector.tensor_copy(f1[1][:].indirect(put1[:, entries_b]), last_b)
-        nc.gpsimd.tensor_tensor(cc[2][:], a[2][:], larger[0][:, whole], ALU.add)
-        for slots, entries in halves:
-            nc.scalar.activation(c5s[2][:, slots], cc[2][:].indirect(take5[:, entries]), COPY)
-            nc.scalar.activation(c6s[2][:, slots], cc[2][:].indirect(take6[:, entries]), COPY)
-        subtract(1)
-        nc.gpsimd.tensor_tensor(gs[2][:, slots_a], c5s[2][:, slots_a], c6s[2][:, slots_a], ALU.subtract)
-        weigh(1, every)
-        weigh(2, slots_a)
-        put_second(3)
+            quarter = slice(lo, lo + QUARTER)
+            scatter(f1[LAST % 2], put1, quarter, last_picked1_a[:, quarter])
+        maximum(2, all_tokens)
+        scatter(f1[LAST % 2], put1, slots_b, last_picked1_b)
+        nc.gpsimd.tensor_tensor(cc[2][:], a[2][:], larger[2][:, all_tokens], ALU.add)
+        for slots in (slots_a, slots_b):
+            look_up(2, slots)
+        subtract(g[1], 1, all_slots)
+        subtract(g[2][:, slots_a], 2, slots_a)
+        weigh(g[1], 1, all_slots)
+        weigh(g[2][:, slots_a], 2, slots_a)
+        put_second(LAST)
 
-        c5 = c5s[last]
-        c6_a, c6_b = c6s[2][:, slots_a], c6s[last][:, slots_b]
-        for c in cols:
-            nc.vector.tensor_tensor(larger[1][:, c], f1[1][:, c], f2[1][:, c], ALU.max)
-        for c in cols:
-            nc.vector.tensor_tensor(cc[2][:, c], a[last][:, c], larger[1][:, c], ALU.add)
-        nc.scalar.activation(c6_a, cc[2][:].indirect(take6[:, entries_a]), COPY)
-        nc.scalar.activation(c6_b, cc[2][:].indirect(take6[:, entries_b]), COPY)
-        late_g = larger[1][:, T - HALF : T]
-        nc.gpsimd.tensor_tensor(late_g, c5s[2][:, slots_b], c6s[2][:, slots_b], ALU.subtract)
-        nc.scalar.activation(gw[:, slots_b, place[2]], late_g, COPY, scale=factor[:, place[2] : place[2] + 1])
-        nc.vector.tensor_copy(c5[:, slots_b], cc[2][:].indirect(take5[:, entries_b]))
-        nc.vector.tensor_tensor(c5[:, slots_a], cc[2][:].indirect(take5[:, entries_a]), c6_a, ALU.subtract)
-        nc.vector.tensor_tensor(c5[:, slots_b], c5[:, slots_b], c6_b, ALU.subtract)
-        r = place[last]
-        for slots, entries in halves:
-            nc.vector.tensor_scalar(gw[:, slots, r], c5[:, slots], factor[:, r : r + 1], None, ALU.mult)
+        for tokens in token_halves:
+            maximum(LAST, tokens)
+        for tokens in token_halves:
+            nc.vector.tensor_tensor(cc[LAST][:, tokens], a[LAST][:, tokens], larger[LAST][:, tokens], ALU.add)
+        last_c6_a, last_c6_b = g[2][:, slots_a], c6[LAST][:, slots_b]
+        gather(last_c6_a, cc[LAST], take6, slots_a)
+        gather(last_c6_b, cc[LAST], take6, slots_b)
+        late_g = larger[LAST][:, T - HALF : T]
+        subtract(late_g, 2, slots_b)
+        weigh(late_g, 2, slots_b)
+        last_g = c5[LAST]
+        nc.vector.tensor_copy(last_g[:, slots_b], cc[LAST][:].indirect(take5[:, entries_of(slots_b)]))
+        nc.vector.tensor_tensor(
+            last_g[:, slots_a], cc[LAST][:].indirect(take5[:, entries_of(slots_a)]), last_c6_a, ALU.subtract
+        )
+        nc.vector.tensor_tensor(last_g[:, slots_b], last_g[:, slots_b], last_c6_b, ALU.subtract)
+        last_place = PLACE[LAST]
+        for slots in (slots_a, slots_b):
+            nc.vector.tensor_scalar(
+                gw[:, slots, last_place], last_g[:, slots], factor[:, last_place : last_place + 1], None, ALU.mult
+            )
+
         gw_codes = keep.tile([P, I], U32, align_bytes=64)
         gw_plane = keep.tile([P, I], U8, align_bytes=64)
-        for slots, entries in halves:
+        for slots in (slots_a, slots_b):
             nc.vector.quantize_mx(
                 out=gw_codes[:, slots].bitcast(FP8X4),
                 scales=gw_plane[:, slots],
                 in_=gw[:, slots, :].rearrange("p i r -> p (i r)"),
             )
-        for h, (slots, entries) in enumerate(halves):
-            for block in range(E // P):
-                rows = slice(block * P, (block + 1) * P)
-                acc = out_banks.tile([P, HALF], F32, name="acc_%d_%d" % (h, block))
+        for half, slots, first_queue in ((0, slots_a, nc.sync), (1, slots_b, nc.scalar)):
+            for block, empty, queue in ((0, nc.scalar.copy, first_queue), (1, nc.vector.tensor_copy, nc.sync)):
+                channels = slice(block * P, (block + 1) * P)
+                acc = out_banks.tile([P, HALF], F32, name="acc_%d_%d" % (half, block))
                 nc.tensor.matmul_mx(
                     out=acc[:],
-                    lhsT=mix_codes[:, rows].bitcast(FP8X4),
-                    lhsT_scale=mix_plane[:, rows],
+                    lhsT=mix_codes[:, channels].bitcast(FP8X4),
+                    lhsT_scale=mix_plane[:, channels],
                     rhs=gw_codes[:, slots].bitcast(FP8X4),
                     rhs_scale=gw_plane[:, slots],
                     start=True,
                     stop=True,
                 )
-                result = keep.tile([P, HALF], F32, name="result_%d_%d" % (h, block))
-                if block == 1:
-                    nc.vector.tensor_copy(out=result[:], in_=acc[:])
-                else:
-                    nc.scalar.copy(out=result[:], in_=acc[:])
-                queue = nc.scalar if (h, block) == (1, 0) else nc.sync
-                queue.dma_start(out=out[rows, slots], in_=result[:])
+                result = keep.tile([P, HALF], F32, name="result_%d_%d" % (half, block))
+                empty(out=result[:], in_=acc[:])
+                queue.dma_start(out=out[channels, slots], in_=result[:])

from contextlib import ExitStack

import concourse.mybir as mybir

D, T, I, Q, E = 512, 1024, 512, 512, 256
FLOPS = 2 * D * Q * T + 2 * Q * E * I

F32 = mybir.dt.float32
BF16 = mybir.dt.bfloat16
I32 = mybir.dt.int32
U32 = mybir.dt.uint32
U16 = mybir.dt.uint16
U8 = mybir.dt.uint8
FP8X4 = mybir.dt.float8_e4m3fn_x4
FP4X4 = mybir.dt.float4_e2m1fn_x4
ALU = mybir.AluOpType
COPY = mybir.ActivationFunctionType.Copy
RELU = mybir.ActivationFunctionType.Relu

P = 128
PACK = 4
BANK = 512
STRIPE = 16
HALF = I // 2
QUARTER = I // 4
PLACE = (0, 2, 3, 1)
LAST = PACK - 1
SCORE_BANKS = 4


def load_scale_rows(queue, plane, scales):
    for quadrant in range(4):
        queue.dma_start(
            out=plane[32 * quadrant : 32 * quadrant + 4, :].bitcast(I32),
            in_=scales[0, 4 * quadrant : 4 * quadrant + 4, :].bitcast(I32),
        )


def entries_of(slots):
    return slice(slots.start // STRIPE, slots.stop // STRIPE)


def tile_attend_passedtwo_one_mixed_kernel(
    tc, query, keys_words, keys_scales, rowf, mix_words, mix_scales, offs, offs2, offs3, offs4, offs5, offs6, out
):
    nc = tc.nc
    all_slots, slots_a, slots_b = slice(0, I), slice(0, HALF), slice(HALF, I)
    all_tokens = slice(0, T)
    token_halves = [slice(b * BANK, (b + 1) * BANK) for b in range(T // BANK)]
    with ExitStack() as ctx:
        lists = ctx.enter_context(tc.tile_pool(name="lists", bufs=1))
        keep = ctx.enter_context(tc.tile_pool(name="keep", bufs=1))
        score_banks = ctx.enter_context(tc.psum_pool(name="score_banks", bufs=SCORE_BANKS))
        out_banks = ctx.enter_context(tc.psum_pool(name="out_banks", bufs=1))

        key_plane = keep.tile([P, T], U8, align_bytes=64)
        mix_plane = keep.tile([P, E], U8, align_bytes=64)
        load_scale_rows(nc.scalar, key_plane, keys_scales)

        q_rows = query.rearrange("(p j) q -> p j q", j=PACK)
        q_raw = [keep.tile([P, 2, Q], F32, name="q_raw_%d" % u) for u in range(2)]
        for u in range(2):
            nc.sync.dma_start(out=q_raw[u][:], in_=q_rows[:, 2 * u : 2 * u + 2, :])
        key_words = [keep.tile([P, 2 * BANK], U8, align_bytes=64, name="key_words_%d" % b) for b in range(T // BANK)]
        for b, words in enumerate(key_words):
            nc.sync.dma_start(
                out=words[:].bitcast(I32), in_=keys_words[0][:, 2 * b * BANK : 2 * (b + 1) * BANK].bitcast(I32)
            )
        take1, take2, put1, put2, take5, take6 = [
            lists.tile([P, I // STRIPE], U16, name="list_%d" % n) for n in range(6)
        ]
        for held, source in ((take1, offs), (put1, offs3), (take2, offs2), (put2, offs4), (take5, offs5), (take6, offs6)):
            nc.sync.dma_start(held[:], source)
        factor = keep.tile([P, PACK], F32)
        nc.sync.dma_start(out=factor[:], in_=rowf.rearrange("(p r) o -> p (r o)", r=PACK))
        mix_codes = keep.tile([P, E], U32, align_bytes=64)
        nc.sync.dma_start(out=mix_codes[:].bitcast(I32), in_=mix_words[0].rearrange("p n t -> p (n t)").bitcast(I32))
        load_scale_rows(nc.sync, mix_plane, mix_scales)

        f1 = [keep.tile([P, T], F32, name="f1_%d" % b) for b in range(2)]
        f2 = [keep.tile([P, T], F32, name="f2_%d" % b) for b in range(2)]
        for window in (f1[0], f2[0], f1[1]):
            nc.vector.memset(window[:], 0.0)
        nc.gpsimd.memset(f2[1][:], 0.0)

        q_cols = [q_raw[u][:].rearrange("p j (m r) -> p m j r", r=PACK) for u in range(2)]
        q_first = keep.tile([P, P, PACK], BF16, align_bytes=64)
        q_rest = keep.tile([P, LAST, P, PACK], BF16, align_bytes=64)
        codes_first = keep.tile([P, P], U32, align_bytes=64)
        plane_first = keep.tile([P, P], U8, align_bytes=64)
        codes_rest = keep.tile([P, LAST * P], U32, align_bytes=64)
        plane_rest = keep.tile([P, LAST * P], U8, align_bytes=64)
        rest_view = q_rest[:].rearrange("p r m j -> p m j r")
        nc.vector.tensor_copy(out=q_first[:, :, 0:2], in_=q_cols[0][:, :, :, 0])
        nc.vector.tensor_copy(out=rest_view[:, :, 0:2, :], in_=q_cols[0][:, :, :, 1:PACK])
        nc.vector.tensor_copy(out=q_first[:, :, 2:4], in_=q_cols[1][:, :, :, 0])
        nc.vector.quantize_mx(
            out=codes_first[:].bitcast(FP8X4), scales=plane_first[:], in_=q_first[:].rearrange("p m j -> p (m j)")
        )
        nc.scalar.copy(out=rest_view[:, :, 2:4, :], in_=q_cols[1][:, :, :, 1:PACK])
        nc.vector.quantize_mx(
            out=codes_rest[:].bitcast(FP8X4), scales=plane_rest[:], in_=q_rest[:].rearrange("p r m j -> p (r m j)")
        )

        a = [keep.tile([P, T], F32, name="a_%d" % s) for s in range(PACK)]
        cc_tiles = [keep.tile([P, T], F32, name="cc_%d" % s) for s in range(LAST)]
        cc = cc_tiles + [cc_tiles[2]]
        partial = keep.tile([P, T], F32)
        excess = cc_tiles[2]
        larger = {2: keep.tile([P, T + QUARTER], F32, name="larger_2"), 3: keep.tile([P, T], F32, name="larger_3")}
        picked1 = [keep.tile([P, I], F32, name="picked1_%d" % s)[:] for s in range(LAST)]
        picked2 = [keep.tile([P, I], F32, name="picked2_%d" % s)[:] for s in range(PACK)]
        last_picked1_a = larger[2][:, T - QUARTER : T + QUARTER]
        c5 = [cc[1][:, all_slots]] + [keep.tile([P, I], F32, name="c5_%d" % s)[:] for s in range(1, PACK)]
        c6 = [keep.tile([P, I], F32, name="c6_%d" % s)[:] for s in range(PACK)]
        g = [picked2[LAST], c6[1], c6[2]]
        last_picked1_b = c6[0][:, slots_b]
        first_gap = [picked2[2], a[LAST][:, token_halves[1]]]
        gw = keep.tile([P, I, PACK], BF16, align_bytes=64)

        def scores(s):
            r = PLACE[s]
            if s == 0:
                codes, plane = codes_first[:], plane_first[:]
                pieces = [
                    (0, 512, nc.scalar.copy),
                    (512, 768, nc.vector.tensor_copy),
                    (768, 896, nc.scalar.copy),
                    (896, 1024, nc.vector.tensor_copy),
                ]
            else:
                codes, plane = codes_rest[:, (r - 1) * P : r * P], plane_rest[:, (r - 1) * P : r * P]
                pieces = [(tokens.start, tokens.stop, nc.scalar.copy) for tokens in token_halves]
            for lo, hi, empty in pieces:
                bank = score_banks.tile([P, hi - lo], F32, name="score")
                nc.tensor.matmul_mx(
                    out=bank[:],
                    lhsT=codes.bitcast(FP8X4),
                    lhsT_scale=plane,
                    rhs=key_words[lo // BANK][:, 2 * (lo % BANK) : 2 * (lo % BANK + hi - lo)].bitcast(FP4X4),
                    rhs_scale=key_plane[:, lo:hi],
                    start=True,
                    stop=True,
                )
                empty(out=a[s][:, lo:hi], in_=bank[:])

        def gather(dense, window, held, slots):
            nc.scalar.activation(dense, window[:].indirect(held[:, entries_of(slots)]), COPY)

        def scatter(window, held, slots, dense):
            nc.vector.tensor_copy(window[:].indirect(held[:, entries_of(slots)]), dense)

        def put_first(s):
            scatter(f1[s % 2], put1, all_slots, picked1[s])

        def put_second(s):
            scatter(f2[s % 2], put2, all_slots, picked2[s])

        def add_first(s):
            nc.gpsimd.tensor_tensor(partial[:], a[s][:], f1[s % 2][:], ALU.add)

        def difference(s, tokens, gap):
            nc.gpsimd.tensor_tensor(gap, f2[s % 2][:, tokens], f1[s % 2][:, tokens], ALU.subtract)

        def clip(tokens, gap):
            nc.scalar.activation(excess[:, tokens], gap, RELU)

        def add_excess(s, tokens):
            nc.gpsimd.tensor_tensor(cc[s][:, tokens], partial[:, tokens], excess[:, tokens], ALU.add)

        def maximum(s, tokens):
            nc.vector.tensor_tensor(larger[s][:, tokens], f1[s % 2][:, tokens], f2[s % 2][:, tokens], ALU.max)

        def look_up(s, slots):
            gather(c5[s][:, slots], cc[s], take5, slots)
            gather(c6[s][:, slots], cc[s], take6, slots)

        def subtract(result, s, slots):
            nc.gpsimd.tensor_tensor(result, c5[s][:, slots], c6[s][:, slots], ALU.subtract)

        def weigh(values, s, slots):
            r = PLACE[s]
            nc.scalar.activation(gw[:, slots, r], values, COPY, scale=factor[:, r : r + 1])

        scores(0)
        nc.vector.tensor_copy(picked1[0][:, slots_a], a[0][:].indirect(take1[:, entries_of(slots_a)]))
        gather(picked1[0][:, slots_b], a[0], take1, slots_b)
        gather(picked2[0], a[0], take2, all_slots)
        scores(1)
        gather(picked1[1], a[1], take1, all_slots)
        gather(picked2[1], a[1], take2, all_slots)
        scores(2)
        gather(picked1[2], a[2], take1, all_slots)

        put_first(0)
        add_first(0)
        put_second(0)
        for tokens, gap in zip(token_halves, first_gap):
            difference(0, tokens, gap)
        for tokens, gap in zip(token_halves, first_gap):
            clip(tokens, gap)
        for tokens in token_halves:
            add_excess(0, tokens)
        gather(picked2[2], a[2], take2, all_slots)
        scores(LAST)
        gather(last_picked1_a, a[LAST], take1, slots_a)
        look_up(0, all_slots)

        put_first(1)
        add_first(1)
        put_second(1)
        difference(1, all_tokens, excess[:])
        clip(all_tokens, excess[:])
        subtract(g[0], 0, all_slots)
        weigh(g[0], 0, all_slots)
        gather(last_picked1_b, a[LAST], take1, slots_b)
        gather(picked2[LAST], a[LAST], take2, all_slots)
        add_excess(1, all_tokens)
        look_up(1, all_slots)

        put_first(2)
        put_second(2)
        for lo in (0, QUARTER):
            quarter = slice(lo, lo + QUARTER)
            scatter(f1[LAST % 2], put1, quarter, last_picked1_a[:, quarter])
        maximum(2, all_tokens)
        scatter(f1[LAST % 2], put1, slots_b, last_picked1_b)
        nc.gpsimd.tensor_tensor(cc[2][:], a[2][:], larger[2][:, all_tokens], ALU.add)
        for slots in (slots_a, slots_b):
            look_up(2, slots)
        subtract(g[1], 1, all_slots)
        subtract(g[2][:, slots_a], 2, slots_a)
        weigh(g[1], 1, all_slots)
        weigh(g[2][:, slots_a], 2, slots_a)
        put_second(LAST)

        for tokens in token_halves:
            maximum(LAST, tokens)
        for tokens in token_halves:
            nc.vector.tensor_tensor(cc[LAST][:, tokens], a[LAST][:, tokens], larger[LAST][:, tokens], ALU.add)
        last_c6_a, last_c6_b = g[2][:, slots_a], c6[LAST][:, slots_b]
        gather(last_c6_a, cc[LAST], take6, slots_a)
        gather(last_c6_b, cc[LAST], take6, slots_b)
        late_g = larger[LAST][:, T - HALF : T]
        subtract(late_g, 2, slots_b)
        weigh(late_g, 2, slots_b)
        last_g = c5[LAST]
        nc.vector.tensor_copy(last_g[:, slots_b], cc[LAST][:].indirect(take5[:, entries_of(slots_b)]))
        nc.vector.tensor_tensor(
            last_g[:, slots_a], cc[LAST][:].indirect(take5[:, entries_of(slots_a)]), last_c6_a, ALU.subtract
        )
        nc.vector.tensor_tensor(last_g[:, slots_b], last_g[:, slots_b], last_c6_b, ALU.subtract)
        last_place = PLACE[LAST]
        for slots in (slots_a, slots_b):
            nc.vector.tensor_scalar(
                gw[:, slots, last_place], last_g[:, slots], factor[:, last_place : last_place + 1], None, ALU.mult
            )

        gw_codes = keep.tile([P, I], U32, align_bytes=64)
        gw_plane = keep.tile([P, I], U8, align_bytes=64)
        for slots in (slots_a, slots_b):
            nc.vector.quantize_mx(
                out=gw_codes[:, slots].bitcast(FP8X4),
                scales=gw_plane[:, slots],
                in_=gw[:, slots, :].rearrange("p i r -> p (i r)"),
            )
        for half, slots, first_queue in ((0, slots_a, nc.sync), (1, slots_b, nc.scalar)):
            for block, empty, queue in ((0, nc.scalar.copy, first_queue), (1, nc.vector.tensor_copy, nc.sync)):
                channels = slice(block * P, (block + 1) * P)
                acc = out_banks.tile([P, HALF], F32, name="acc_%d_%d" % (half, block))
                nc.tensor.matmul_mx(
                    out=acc[:],
                    lhsT=mix_codes[:, channels].bitcast(FP8X4),
                    lhsT_scale=mix_plane[:, channels],
                    rhs=gw_codes[:, slots].bitcast(FP8X4),
                    rhs_scale=gw_plane[:, slots],
                    start=True,
                    stop=True,
                )
                result = keep.tile([P, HALF], F32, name="result_%d_%d" % (half, block))
                empty(out=result[:], in_=acc[:])
                queue.dma_start(out=out[channels, slots], in_=result[:])
